import numpy as np
import ml_dtypes


def mxq(x, axis, fmt="e4m3"):
    dtype, down = {"e4m3": (ml_dtypes.float8_e4m3fn, 7), "e5m2": (ml_dtypes.float8_e5m2, 14)}[fmt]
    v = np.moveaxis(np.asarray(x, np.float32).astype(ml_dtypes.bfloat16).astype(np.float64), axis, -1)
    blocks = v.reshape(v.shape[:-1] + (-1, 32))
    amax = np.abs(blocks).max(-1, keepdims=True)
    byte = np.maximum(np.where(amax > 0, np.frexp(amax)[1] - 1 + 127, 0) - down, 1)
    scale = np.exp2(byte - 127.0)
    codes = (blocks / scale).astype(np.float32).astype(dtype).astype(np.float64)
    return np.moveaxis((codes * scale).reshape(v.shape), -1, axis)


WIDE = False


def mx_kscale(k):
    if not WIDE:
        return np.ones(k)
    levels = np.array([10, -10, 5, -5, 0])
    if k % 512:
        return np.exp2(np.random.permutation(np.resize(levels, k // 32))).repeat(32)
    a = np.empty((k // 512, 16))
    for p in range(k // 512):
        a[p, :8] = np.random.permutation(np.resize(levels, 8))
        for g in range(8):
            far = levels[np.abs(levels - a[p, g]) >= 10]
            a[p, g + 8] = far[np.random.randint(len(far))]
    return np.exp2(a.ravel()).repeat(32)


def f64(x):
    return np.asarray(x).astype(np.float64)


def striped(idx):
    return np.tile(idx.reshape(-1, 16).T, (8, 1)).astype(np.uint16)


def unstriped(offs):
    return offs[:16].T.reshape(-1).astype(np.int64)


def pack_weight(w):
    k, n = w.shape
    w = f64(np.asarray(w, np.float32).astype(ml_dtypes.bfloat16)).reshape(k // 32, 32, n)
    amax = np.abs(w).max(1)
    byte = np.clip(np.where(amax > 0, np.frexp(amax)[1] - 1 + 127 - 7, 1), 1, 254)
    scaled = (w * np.exp2(127.0 - byte)[:, None, :]).reshape(k, n).astype(np.float32)
    words = np.ascontiguousarray(scaled.reshape(k // 512, 128, 4, n).transpose(0, 1, 3, 2)).astype(ml_dtypes.float8_e4m3fn).view(np.uint8)
    return words, np.ascontiguousarray(byte.astype(np.uint8).reshape(k // 512, 16, n))


def unpack_weight(words, scales):
    g, p, n, _ = words.shape
    vals = np.ascontiguousarray(words).view(ml_dtypes.float8_e4m3fn).astype(np.float64) * np.repeat(np.exp2(scales.astype(np.float64) - 127.0), 8, axis=1)[..., None]
    return vals.transpose(0, 1, 3, 2).reshape(g * 512, n)


def planes(y):
    n, m = y.shape
    v = y.astype(np.float32).astype(ml_dtypes.bfloat16).astype(np.float64).reshape(n // 32, 32, m)
    top = np.abs(v).max(1)
    byte = np.clip(np.where(top > 0, np.frexp(top)[1] - 1 + 127 - 7, 1), 1, 254)
    codes = (v * np.exp2(127.0 - byte)[:, None, :]).reshape(n, m).astype(np.float32).astype(ml_dtypes.float8_e4m3fn).view(np.uint8)
    words = codes.reshape(n // 512, 128, 4, m).transpose(0, 1, 3, 2)
    return np.ascontiguousarray(words), np.ascontiguousarray(byte.astype(np.uint8).reshape(n // 512, 16, m))


K, T, S, N, H, W, U = 512, 1024, 512, 512, 512, 1024, 1024


def setup_inputs():
    n = np.random.standard_normal
    s = mx_kscale(K)[:, None]
    u = mx_kscale(H)
    packed_xT = pack_weight(n((K, T)) * s)
    packed_eT = pack_weight(n((K, W)) * s)
    return {
        "x_words": packed_xT[0],
        "x_scales": packed_xT[1],
        "w1": (n((K, N)) / np.sqrt(K) / s).astype(np.float32),
        "w2": (n((K, N)) / np.sqrt(K) / s).astype(np.float32),
        "e_words": packed_eT[0],
        "e_scales": packed_eT[1],
        "w3": (n((K, N)) / np.sqrt(K) / s).astype(np.float32),
        "unit": (np.random.uniform(0.6, 1.4, (H, 1)) * u[:, None]).astype(np.float32),
        "w4": (n((H, N)) / np.sqrt(H) / u[:, None]).astype(np.float32),
        "offs": striped(np.random.permutation(T)[:S]),
        "sup": striped(np.random.permutation(W)[:S]),
        "itm": striped(np.random.permutation(np.concatenate([np.arange(S), np.random.randint(0, S, U - S)]))),
        "sp": striped(np.random.permutation(np.concatenate([np.arange(S), np.random.randint(0, S, U - S)]))),
        "sb2": striped(np.random.permutation(np.concatenate([np.arange(S), np.random.randint(0, S, U - S)]))),
    }


def reference(x_words, x_scales, w1, w2, e_words, e_scales, w3, unit, w4, offs, sup, itm, sp, sb2):
    xq = unpack_weight(x_words, x_scales)[:, unstriped(offs)]
    y = mxq(f64(w1), 0, "e4m3").T @ xq
    yi2 = y[:, unstriped(itm)]
    e_sup = unpack_weight(e_words, e_scales)[:, unstriped(sup)]
    ye = mxq(f64(w3), 0, "e4m3").T @ e_sup
    es = ye[:, unstriped(sp)]
    avl = yi2 * es
    z1 = mxq(f64(w2), 0, "e4m3").T @ xq
    zi2 = z1[:, unstriped(itm)]
    gap2 = avl - zi2
    ysb = y[:, unstriped(sb2)]
    hid = f64(unit) * (gap2 * ysb)
    out_0 = mxq(f64(w4), 0, "e4m3").T @ mxq(hid, 0, "e4m3")
    return (out_0,) + planes(out_0)

@@ -1,0 +1,199 @@
+from contextlib import ExitStack
+
+import concourse.mybir as mybir
+
+F32 = mybir.dt.float32
+BF16 = mybir.dt.bfloat16
+I32 = mybir.dt.int32
+U32 = mybir.dt.uint32
+U16 = mybir.dt.uint16
+U8 = mybir.dt.uint8
+FP8X4 = mybir.dt.float8_e4m3fn_x4
+MULT = mybir.AluOpType.mult
+ADD = mybir.AluOpType.add
+COPY = mybir.ActivationFunctionType.Copy
+
+P = 128
+PACK = 4
+TABLE = 1024
+PICKED = 512
+ORDERS = 1024
+CHUNKS = (256, 256, 256, 256)
+FLOPS = 2 * 512 * 512 * (3 * PICKED + ORDERS)
+
+
+def tile_picked_yinvent_sub_po_kernel(tc, x_words, x_scales, w1, w2, e_words, e_scales, w3, unit, w4, offs, sup, itm, sp, sb2, out_0, out_1, out_2):
+    nc = tc.nc
+    with ExitStack() as ctx:
+        keep = ctx.enter_context(tc.tile_pool(name="keep", bufs=1))
+        psum = ctx.enter_context(tc.psum_pool(name="psum", bufs=4))
+
+        def load_list(name, src):
+            t = keep.tile(list(src.shape), U16, name=name)
+            nc.sync.dma_start(t[:], src)
+            return t
+
+        def load_words(name, src):
+            t = keep.tile([P, TABLE], U32, name=name, align_bytes=64)
+            nc.sync.dma_start(t[:].bitcast(I32), src[0].rearrange("p c r -> p (c r)").bitcast(I32))
+            return t
+
+        def load_scales(name, src, queue):
+            t = keep.tile([P, TABLE], U8, name=name, align_bytes=64)
+            nc.vector.memset(t[:].bitcast(I32), 0)
+            for q in range(4):
+                queue.dma_start(t[32 * q : 32 * q + 4, :].bitcast(I32), src[0, 4 * q : 4 * q + 4, :].bitcast(I32))
+            return t
+
+        def load_weight(name, src, c0, c1):
+            t = keep.tile([P, PACK, c1 - c0], F32, name=name)
+            nc.sync.dma_start(t[:], src.rearrange("(p j) c -> p j c", j=PACK)[:, :, c0:c1])
+            return t
+
+        def gather_codes(name, table, dtype, lst):
+            t = keep.tile([P, PICKED], dtype, name=name, align_bytes=64)
+            nc.vector.tensor_copy(t[:], table[:].indirect(lst[:]))
+            return t
+
+        def deal(engine, dealt, raw, m0, m1):
+            dst = dealt[:].rearrange("p (t m j) -> p m j t", t=PACK, j=PACK)[:, m0:m1, :, :]
+            src = raw.rearrange("p j (m t) -> p m j t", t=PACK)
+            if engine == "scalar":
+                nc.scalar.activation(dst, src, COPY)
+            else:
+                nc.vector.tensor_copy(dst, src)
+
+        def quantize(name, values, width):
+            codes = keep.tile([P, width], U32, name=name + "_codes", align_bytes=64)
+            scales = keep.tile([P, width], U8, name=name + "_scales", align_bytes=64)
+            nc.vector.quantize_mx(out=codes[:].bitcast(FP8X4), scales=scales[:], in_=values)
+            return codes, scales
+
+        def product(dst, weight, t, codes, scales):
+            cols = slice(P * t, P * (t + 1))
+            nc.tensor.matmul_mx(out=dst, lhsT=weight[0][:, cols].bitcast(FP8X4), lhsT_scale=weight[1][:, cols],
+                                rhs=codes.bitcast(FP8X4), rhs_scale=scales, start=True, stop=True)
+
+        def first_layer(name, weight, codes, scales, factor):
+            tiles = []
+            for t in range(PACK):
+                bank = psum.tile([P, PICKED], F32, name="first_bank")
+                product(bank[:], weight, t, codes[:], scales[:])
+                res = keep.tile([P, PICKED], F32, name="%s%d" % (name, t))
+                if factor is None:
+                    nc.scalar.activation(res[:], bank[:], COPY)
+                else:
+                    nc.scalar.activation(res[:], bank[:], COPY, scale=factor[:, t : t + 1])
+                tiles.append(res)
+            return tiles
+
+        offs_t = load_list("offs", offs)
+        xw = load_words("xw", x_words)
+        xs = load_scales("xs", x_scales, nc.sync)
+        w1a = load_weight("w1a", w1, 0, 256)
+        w1b = load_weight("w1b", w1, 256, 512)
+        sup_t = load_list("sup", sup)
+        ew = load_words("ew", e_words)
+        w3r = load_weight("w3r", w3, 0, 512)
+        es = load_scales("es", e_scales, nc.sync)
+        u = keep.tile([P, PACK], F32, name="u")
+        nc.sync.dma_start(u[:], unit.rearrange("(p t) o -> p (t o)", t=PACK))
+        w2r = load_weight("w2r", w2, 0, 512)
+        itm_t = load_list("itm", itm)
+        sb2_t = load_list("sb2", sb2)
+        sp_t = load_list("sp", sp)
+        w4r = load_weight("w4r", w4, 0, 512)
+
+        dealt = [keep.tile([P, 512 * PACK], BF16, name="dealt%d" % i, align_bytes=64) for i in range(4)]
+
+        xw_p = gather_codes("xw_p", xw, U32, offs_t)
+        xs_p = gather_codes("xs_p", xs, U8, offs_t)
+        deal("scalar", dealt[0], w1a[:], 0, 64)
+        deal("vector", dealt[0], w1b[:], 64, 128)
+        q1 = quantize("q1", dealt[0][:], 512)
+        ew_p = gather_codes("ew_p", ew, U32, sup_t)
+        es_p = gather_codes("es_p", es, U8, sup_t)
+        neg_u = keep.tile([P, PACK], F32, name="neg_u")
+        nc.vector.tensor_scalar(neg_u[:], u[:], -1.0, None, MULT)
+        y = first_layer("y", q1, xw_p, xs_p, None)
+        deal("scalar", dealt[1], w3r[:, :, 0:256], 0, 64)
+        deal("vector", dealt[1], w3r[:, :, 256:512], 64, 128)
+        q3 = quantize("q3", dealt[1][:], 512)
+        ye = first_layer("ye", q3, ew_p, es_p, u)
+        deal("scalar", dealt[2], w2r[:, :, 0:256], 0, 64)
+        deal("vector", dealt[2], w2r[:, :, 256:512], 64, 128)
+        q2 = quantize("q2", dealt[2][:], 512)
+        z = first_layer("z", q2, xw_p, xs_p, neg_u)
+
+        out_codes = keep.tile([P, ORDERS], U32, name="out_codes", align_bytes=64)
+        out_scales = keep.tile([P, ORDERS], U8, name="out_scales", align_bytes=64)
+        out_rows = out_0.rearrange("(p t) r -> p t r", t=PACK)
+        out_words = out_1[0].rearrange("p c r -> p (c r)").bitcast(I32)
+
+        starts = [sum(CHUNKS[:c]) for c in range(len(CHUNKS))]
+        state = {}
+
+        def look_up(c):
+            n, r0 = CHUNKS[c], starts[c]
+            cols = slice(r0 // 16, (r0 + n) // 16)
+            a = keep.tile([P, PACK, n], F32, name="a%d" % c)
+            g = keep.tile([P, PACK, n], F32, name="g%d" % c)
+            for t in range(PACK):
+                nc.scalar.activation(a[:, t, :], y[t][:].indirect(itm_t[:, cols]), COPY)
+            for t in range(PACK):
+                nc.scalar.activation(g[:, t, :], y[t][:].indirect(sb2_t[:, cols]), COPY)
+            state[c] = (a, g)
+
+        def combine(c):
+            n, r0 = CHUNKS[c], starts[c]
+            cols = slice(r0 // 16, (r0 + n) // 16)
+            a, g = state[c]
+            b = keep.tile([P, PACK, n], F32, name="b%d" % c)
+            gap = keep.tile([P, PACK, n], F32, name="gap%d" % c)
+            for t in range(PACK):
+                nc.vector.tensor_tensor(b[:, t, :], ye[t][:].indirect(sp_t[:, cols]), a[:, t, :], MULT)
+            for t in range(PACK):
+                nc.vector.tensor_tensor(gap[:, t, :], z[t][:].indirect(itm_t[:, cols]), b[:, t, :], ADD)
+            hid = keep.tile([P, n * PACK], BF16, name="hid%d" % c, align_bytes=64)
+            nc.vector.tensor_tensor(hid[:].rearrange("p (c i t) -> p c t i", i=4, t=PACK),
+                                    gap[:].rearrange("p t (c i) -> p c t i", i=4),
+                                    g[:].rearrange("p t (c i) -> p c t i", i=4), MULT)
+            state[c] = hid
+
+        def last_product(c, q4):
+            n, r0 = CHUNKS[c], starts[c]
+            codes, scales = quantize("hq%d" % c, state[c][:], n)
+            res = keep.tile([P, PACK, n], F32, name="res%d" % c)
+            per_bank = 512 // n
+            for t0 in range(0, PACK, per_bank):
+                bank = psum.tile([P, per_bank, n], F32, name="last_bank")
+                for t in range(per_bank):
+                    product(bank[:, t, :], q4, t0 + t, codes[:], scales[:])
+                nc.scalar.activation(res[:, t0 : t0 + per_bank, :], bank[:], COPY)
+            nc.sync.dma_start(out_rows[:, :, r0 : r0 + n], res[:])
+            state[c] = res
+
+        def planes(c):
+            n, r0 = CHUNKS[c], starts[c]
+            rounded = keep.tile([P, n * PACK], BF16, name="rounded%d" % c, align_bytes=64)
+            nc.vector.tensor_copy(rounded[:].rearrange("p (c i t) -> p c t i", i=4, t=PACK),
+                                  state[c][:].rearrange("p t (c i) -> p c t i", i=4))
+            nc.vector.quantize_mx(out=out_codes[:, r0 : r0 + n].bitcast(FP8X4), scales=out_scales[:, r0 : r0 + n], in_=rounded[:])
+            nc.sync.dma_start(out_words[:, r0 : r0 + n], out_codes[:, r0 : r0 + n].bitcast(I32))
+
+        look_up(0)
+        deal("scalar", dealt[3], w4r[:], 0, 128)
+        q4 = quantize("q4", dealt[3][:], 512)
+        count = len(CHUNKS)
+        for c in range(count + 2):
+            if c + 1 < count:
+                look_up(c + 1)
+            if c < count:
+                combine(c)
+            if 1 <= c <= count:
+                last_product(c - 1, q4)
+            if c >= 2:
+                planes(c - 2)
+        for q in range(4):
+            queue = nc.sync if q % 2 == 0 else nc.scalar
+            queue.dma_start(out_2[0, 4 * q : 4 * q + 4, :].bitcast(I32), out_scales[32 * q : 32 * q + 4, :].bitcast(I32))

@@ -18,7 +18,8 @@ PACK = 4
 TABLE = 1024
 PICKED = 512
 ORDERS = 1024
-CHUNKS = (256, 256, 256, 256)
+CHUNKS = (256, 384, 256, 128)
+RING = 3
 FLOPS = 2 * 512 * 512 * (3 * PICKED + ORDERS)
 
 
@@ -50,8 +51,8 @@ def tile_picked_yinvent_sub_po_kernel(tc, x_words, x_scales, w1, w2, e_words, e_
             nc.sync.dma_start(t[:], src.rearrange("(p j) c -> p j c", j=PACK)[:, :, c0:c1])
             return t
 
-        def gather_codes(name, table, dtype, lst):
-            t = keep.tile([P, PICKED], dtype, name=name, align_bytes=64)
+        def gather_codes(name, table, dtype, lst, tag=None):
+            t = keep.tile([P, PICKED], dtype, name=name, tag=tag or name, align_bytes=64)
             nc.vector.tensor_copy(t[:], table[:].indirect(lst[:]))
             return t
 
@@ -63,9 +64,10 @@ def tile_picked_yinvent_sub_po_kernel(tc, x_words, x_scales, w1, w2, e_words, e_
             else:
                 nc.vector.tensor_copy(dst, src)
 
-        def quantize(name, values, width):
-            codes = keep.tile([P, width], U32, name=name + "_codes", align_bytes=64)
-            scales = keep.tile([P, width], U8, name=name + "_scales", align_bytes=64)
+        def quantize(name, values, width, tags=None):
+            tags = tags or (name + "_codes", name + "_scales")
+            codes = keep.tile([P, width], U32, name=name + "_codes", tag=tags[0], align_bytes=64)
+            scales = keep.tile([P, width], U8, name=name + "_scales", tag=tags[1], align_bytes=64)
             nc.vector.quantize_mx(out=codes[:].bitcast(FP8X4), scales=scales[:], in_=values)
             return codes, scales
 
@@ -88,41 +90,40 @@ def tile_picked_yinvent_sub_po_kernel(tc, x_words, x_scales, w1, w2, e_words, e_
             return tiles
 
         offs_t = load_list("offs", offs)
-        xw = load_words("xw", x_words)
-        xs = load_scales("xs", x_scales, nc.sync)
         w1a = load_weight("w1a", w1, 0, 256)
+        xs = load_scales("xs", x_scales, nc.sync)
+        xw = load_words("xw", x_words)
         w1b = load_weight("w1b", w1, 256, 512)
-        sup_t = load_list("sup", sup)
         ew = load_words("ew", e_words)
-        w3r = load_weight("w3r", w3, 0, 512)
+        sup_t = load_list("sup", sup)
         es = load_scales("es", e_scales, nc.sync)
-        u = keep.tile([P, PACK], F32, name="u")
-        nc.sync.dma_start(u[:], unit.rearrange("(p t) o -> p (t o)", t=PACK))
+        w3r = load_weight("w3r", w3, 0, 512)
         w2r = load_weight("w2r", w2, 0, 512)
         itm_t = load_list("itm", itm)
-        sb2_t = load_list("sb2", sb2)
+        u = keep.tile([P, PACK], F32, name="u")
+        nc.sync.dma_start(u[:], unit.rearrange("(p t) o -> p (t o)", t=PACK))
         sp_t = load_list("sp", sp)
+        sb2_t = load_list("sb2", sb2)
         w4r = load_weight("w4r", w4, 0, 512)
 
-        dealt = [keep.tile([P, 512 * PACK], BF16, name="dealt%d" % i, align_bytes=64) for i in range(4)]
+        dealt = [keep.tile([P, 512 * PACK], BF16, name="dealt%d" % i, tag="dealt%d" % i, align_bytes=64) for i in range(4)]
 
-        xw_p = gather_codes("xw_p", xw, U32, offs_t)
         xs_p = gather_codes("xs_p", xs, U8, offs_t)
+        xw_p = gather_codes("xw_p", xw, U32, offs_t)
         deal("scalar", dealt[0], w1a[:], 0, 64)
-        deal("vector", dealt[0], w1b[:], 64, 128)
+        deal("vector", dealt[0], w1b[:, :, 0:160], 64, 104)
+        deal("scalar", dealt[0], w1b[:, :, 160:256], 104, 128)
         q1 = quantize("q1", dealt[0][:], 512)
-        ew_p = gather_codes("ew_p", ew, U32, sup_t)
+        ew_p = gather_codes("ew_p", ew, U32, sup_t, "dealt0")
         es_p = gather_codes("es_p", es, U8, sup_t)
         neg_u = keep.tile([P, PACK], F32, name="neg_u")
         nc.vector.tensor_scalar(neg_u[:], u[:], -1.0, None, MULT)
         y = first_layer("y", q1, xw_p, xs_p, None)
-        deal("scalar", dealt[1], w3r[:, :, 0:256], 0, 64)
-        deal("vector", dealt[1], w3r[:, :, 256:512], 64, 128)
+        deal("vector", dealt[1], w3r[:], 0, 128)
         q3 = quantize("q3", dealt[1][:], 512)
         ye = first_layer("ye", q3, ew_p, es_p, u)
-        deal("scalar", dealt[2], w2r[:, :, 0:256], 0, 64)
-        deal("vector", dealt[2], w2r[:, :, 256:512], 64, 128)
-        q2 = quantize("q2", dealt[2][:], 512)
+        deal("vector", dealt[2], w2r[:], 0, 128)
+        q2 = quantize("q2", dealt[2][:], 512, ("ring2", "ring1"))
         z = first_layer("z", q2, xw_p, xs_p, neg_u)
 
         out_codes = keep.tile([P, ORDERS], U32, name="out_codes", align_bytes=64)
@@ -133,65 +134,82 @@ def tile_picked_yinvent_sub_po_kernel(tc, x_words, x_scales, w1, w2, e_words, e_
         starts = [sum(CHUNKS[:c]) for c in range(len(CHUNKS))]
         state = {}
 
+        def list_cols(c):
+            return slice(starts[c] // 16, (starts[c] + CHUNKS[c]) // 16)
+
         def look_up(c):
-            n, r0 = CHUNKS[c], starts[c]
-            cols = slice(r0 // 16, (r0 + n) // 16)
-            a = keep.tile([P, PACK, n], F32, name="a%d" % c)
-            g = keep.tile([P, PACK, n], F32, name="g%d" % c)
-            for t in range(PACK):
-                nc.scalar.activation(a[:, t, :], y[t][:].indirect(itm_t[:, cols]), COPY)
-            for t in range(PACK):
-                nc.scalar.activation(g[:, t, :], y[t][:].indirect(sb2_t[:, cols]), COPY)
-            state[c] = (a, g)
+            for name, lst, slot in (("a", itm_t, 2 * c), ("g", sb2_t, 2 * c + 1)):
+                picked = keep.tile([P, PACK, CHUNKS[c]], F32, name="%s%d" % (name, c), tag="ring%d" % (slot % RING), align_bytes=64)
+                for t in range(PACK):
+                    nc.scalar.activation(picked[:, t, :], y[t][:].indirect(lst[:, list_cols(c)]), COPY)
+                state[name, c] = picked
 
-        def combine(c):
-            n, r0 = CHUNKS[c], starts[c]
-            cols = slice(r0 // 16, (r0 + n) // 16)
-            a, g = state[c]
-            b = keep.tile([P, PACK, n], F32, name="b%d" % c)
-            gap = keep.tile([P, PACK, n], F32, name="gap%d" % c)
+        def times_supplier(c):
+            b = keep.tile([P, PACK, CHUNKS[c]], F32, name="b%d" % c)
             for t in range(PACK):
-                nc.vector.tensor_tensor(b[:, t, :], ye[t][:].indirect(sp_t[:, cols]), a[:, t, :], MULT)
+                nc.vector.tensor_tensor(b[:, t, :], ye[t][:].indirect(sp_t[:, list_cols(c)]), state["a", c][:, t, :], MULT)
+            state["b", c] = b
+
+        def less_second(c):
+            gap = keep.tile([P, PACK, CHUNKS[c]], F32, name="gap%d" % c)
             for t in range(PACK):
-                nc.vector.tensor_tensor(gap[:, t, :], z[t][:].indirect(itm_t[:, cols]), b[:, t, :], ADD)
-            hid = keep.tile([P, n * PACK], BF16, name="hid%d" % c, align_bytes=64)
+                nc.vector.tensor_tensor(gap[:, t, :], z[t][:].indirect(itm_t[:, list_cols(c)]), state["b", c][:, t, :], ADD)
+            state["gap", c] = gap
+
+        def times_substitute(c):
+            hid = keep.tile([P, CHUNKS[c] * PACK], BF16, name="hid%d" % c, align_bytes=64)
             nc.vector.tensor_tensor(hid[:].rearrange("p (c i t) -> p c t i", i=4, t=PACK),
-                                    gap[:].rearrange("p t (c i) -> p c t i", i=4),
-                                    g[:].rearrange("p t (c i) -> p c t i", i=4), MULT)
-            state[c] = hid
+                                    state["gap", c][:].rearrange("p t (c i) -> p c t i", i=4),
+                                    state["g", c][:].rearrange("p t (c i) -> p c t i", i=4), MULT)
+            state["hid", c] = hid
 
-        def last_product(c, q4):
+        def last_product(c):
             n, r0 = CHUNKS[c], starts[c]
-            codes, scales = quantize("hq%d" % c, state[c][:], n)
+            codes, scales = quantize("hq%d" % c, state["hid", c][:], n)
             res = keep.tile([P, PACK, n], F32, name="res%d" % c)
             per_bank = 512 // n
             for t0 in range(0, PACK, per_bank):
                 bank = psum.tile([P, per_bank, n], F32, name="last_bank")
                 for t in range(per_bank):
-                    product(bank[:, t, :], q4, t0 + t, codes[:], scales[:])
+                    for lo, hi in ((0, min(n, 256)), (256, n)):
+                        if hi > lo:
+                            product(bank[:, t, lo:hi], q4, t0 + t, codes[:, lo:hi], scales[:, lo:hi])
                 nc.scalar.activation(res[:, t0 : t0 + per_bank, :], bank[:], COPY)
             nc.sync.dma_start(out_rows[:, :, r0 : r0 + n], res[:])
-            state[c] = res
+            state["res", c] = res
+
+        def round_result(c, values):
+            rounded = keep.tile([P, CHUNKS[c] * PACK], BF16, name="rounded%d" % c, align_bytes=64)
+            dst = rounded[:].rearrange("p (c i t) -> p c t i", i=4, t=PACK)
+            src = values[:].rearrange("p t (c i) -> p c t i", i=4)
+            if c < 2:
+                nc.scalar.activation(dst, src, COPY)
+            else:
+                nc.vector.tensor_copy(dst, src)
+            state["rounded", c] = rounded
 
         def planes(c):
             n, r0 = CHUNKS[c], starts[c]
-            rounded = keep.tile([P, n * PACK], BF16, name="rounded%d" % c, align_bytes=64)
-            nc.vector.tensor_copy(rounded[:].rearrange("p (c i t) -> p c t i", i=4, t=PACK),
-                                  state[c][:].rearrange("p t (c i) -> p c t i", i=4))
-            nc.vector.quantize_mx(out=out_codes[:, r0 : r0 + n].bitcast(FP8X4), scales=out_scales[:, r0 : r0 + n], in_=rounded[:])
+            nc.vector.quantize_mx(out=out_codes[:, r0 : r0 + n].bitcast(FP8X4), scales=out_scales[:, r0 : r0 + n], in_=state["rounded", c][:])
             nc.sync.dma_start(out_words[:, r0 : r0 + n], out_codes[:, r0 : r0 + n].bitcast(I32))
 
-        look_up(0)
-        deal("scalar", dealt[3], w4r[:], 0, 128)
+        deal("vector", dealt[3], w4r[:], 0, 128)
         q4 = quantize("q4", dealt[3][:], 512)
         count = len(CHUNKS)
+        look_up(0)
         for c in range(count + 2):
             if c + 1 < count:
                 look_up(c + 1)
             if c < count:
-                combine(c)
+                times_supplier(c)
             if 1 <= c <= count:
-                last_product(c - 1, q4)
+                last_product(c - 1)
+            if c < count:
+                less_second(c)
+            if c >= 2:
+                round_result(c - 2, state["res", c - 2])
+            if c < count:
+                times_substitute(c)
             if c >= 2:
                 planes(c - 2)
         for q in range(4):

@@ -19,6 +19,7 @@ TABLE = 1024
 PICKED = 512
 ORDERS = 1024
 CHUNKS = (256, 384, 256, 128)
+SPARE = 0
 RING = 3
 FLOPS = 2 * 512 * 512 * (3 * PICKED + ORDERS)
 
@@ -81,11 +82,11 @@ def tile_picked_yinvent_sub_po_kernel(tc, x_words, x_scales, w1, w2, e_words, e_
             for t in range(PACK):
                 bank = psum.tile([P, PICKED], F32, name="first_bank")
                 product(bank[:], weight, t, codes[:], scales[:])
-                res = keep.tile([P, PICKED], F32, name="%s%d" % (name, t))
+                res = keep.tile([P, PICKED + SPARE], F32, name="%s%d" % (name, t))
                 if factor is None:
-                    nc.scalar.activation(res[:], bank[:], COPY)
+                    nc.scalar.activation(res[:, :PICKED], bank[:], COPY)
                 else:
-                    nc.scalar.activation(res[:], bank[:], COPY, scale=factor[:, t : t + 1])
+                    nc.scalar.activation(res[:, :PICKED], bank[:], COPY, scale=factor[:, t : t + 1])
                 tiles.append(res)
             return tiles
 
@@ -98,13 +99,16 @@ def tile_picked_yinvent_sub_po_kernel(tc, x_words, x_scales, w1, w2, e_words, e_
         sup_t = load_list("sup", sup)
         es = load_scales("es", e_scales, nc.sync)
         w3r = load_weight("w3r", w3, 0, 512)
-        w2r = load_weight("w2r", w2, 0, 512)
+        w3a, w3b = w3r[:, :, 0:256], w3r[:, :, 256:512]
         itm_t = load_list("itm", itm)
+        w2r = load_weight("w2r", w2, 0, 512)
+        w2a, w2b = w2r[:, :, 0:256], w2r[:, :, 256:512]
         u = keep.tile([P, PACK], F32, name="u")
         nc.sync.dma_start(u[:], unit.rearrange("(p t) o -> p (t o)", t=PACK))
         sp_t = load_list("sp", sp)
         sb2_t = load_list("sb2", sb2)
         w4r = load_weight("w4r", w4, 0, 512)
+        w4a, w4b = w4r[:, :, 0:256], w4r[:, :, 256:512]
 
         dealt = [keep.tile([P, 512 * PACK], BF16, name="dealt%d" % i, tag="dealt%d" % i, align_bytes=64) for i in range(4)]
 
@@ -143,24 +147,32 @@ def tile_picked_yinvent_sub_po_kernel(tc, x_words, x_scales, w1, w2, e_words, e_
                 for t in range(PACK):
                     nc.scalar.activation(picked[:, t, :], y[t][:].indirect(lst[:, list_cols(c)]), COPY)
                 state[name, c] = picked
+            if c >= len(CHUNKS) - 0:
+                second = keep.tile([P, PACK, CHUNKS[c]], F32, name="second%d" % c, tag="b%d" % (c - 2))
+                for t in range(PACK):
+                    nc.scalar.activation(second[:, t, :], z[t][:].indirect(itm_t[:, list_cols(c)]), COPY)
+                state["second", c] = second
 
         def times_supplier(c):
-            b = keep.tile([P, PACK, CHUNKS[c]], F32, name="b%d" % c)
+            b = keep.tile([P, PACK, CHUNKS[c]], F32, name="b%d" % c, tag="b%d" % c)
             for t in range(PACK):
                 nc.vector.tensor_tensor(b[:, t, :], ye[t][:].indirect(sp_t[:, list_cols(c)]), state["a", c][:, t, :], MULT)
             state["b", c] = b
 
         def less_second(c):
             gap = keep.tile([P, PACK, CHUNKS[c]], F32, name="gap%d" % c)
-            for t in range(PACK):
-                nc.vector.tensor_tensor(gap[:, t, :], z[t][:].indirect(itm_t[:, list_cols(c)]), state["b", c][:, t, :], ADD)
+            if c >= len(CHUNKS) - 0:
+                nc.vector.tensor_tensor(gap[:], state["second", c][:], state["b", c][:], ADD)
+            else:
+                for t in range(PACK):
+                    nc.vector.tensor_tensor(gap[:, t, :], z[t][:].indirect(itm_t[:, list_cols(c)]), state["b", c][:, t, :], ADD)
             state["gap", c] = gap
 
         def times_substitute(c):
             hid = keep.tile([P, CHUNKS[c] * PACK], BF16, name="hid%d" % c, align_bytes=64)
-            nc.vector.tensor_tensor(hid[:].rearrange("p (c i t) -> p c t i", i=4, t=PACK),
-                                    state["gap", c][:].rearrange("p t (c i) -> p c t i", i=4),
-                                    state["g", c][:].rearrange("p t (c i) -> p c t i", i=4), MULT)
+            nc.vector.tensor_tensor(hid[:].rearrange("p (c i t) -> p c t i", i=2, t=PACK),
+                                    state["gap", c][:].rearrange("p t (c i) -> p c t i", i=2),
+                                    state["g", c][:].rearrange("p t (c i) -> p c t i", i=2), MULT)
             state["hid", c] = hid
 
         def last_product(c):
@@ -171,17 +183,17 @@ def tile_picked_yinvent_sub_po_kernel(tc, x_words, x_scales, w1, w2, e_words, e_
             for t0 in range(0, PACK, per_bank):
                 bank = psum.tile([P, per_bank, n], F32, name="last_bank")
                 for t in range(per_bank):
-                    for lo, hi in ((0, min(n, 256)), (256, n)):
+                    for lo, hi in (((0, 256), (256, n)) if n == 384 else ((0, n),)):
                         if hi > lo:
                             product(bank[:, t, lo:hi], q4, t0 + t, codes[:, lo:hi], scales[:, lo:hi])
                 nc.scalar.activation(res[:, t0 : t0 + per_bank, :], bank[:], COPY)
-            nc.sync.dma_start(out_rows[:, :, r0 : r0 + n], res[:])
+                nc.sync.dma_start(out_rows[:, t0 : t0 + per_bank, r0 : r0 + n], res[:, t0 : t0 + per_bank, :])
             state["res", c] = res
 
         def round_result(c, values):
             rounded = keep.tile([P, CHUNKS[c] * PACK], BF16, name="rounded%d" % c, align_bytes=64)
-            dst = rounded[:].rearrange("p (c i t) -> p c t i", i=4, t=PACK)
-            src = values[:].rearrange("p t (c i) -> p c t i", i=4)
+            dst = rounded[:].rearrange("p (c i t) -> p c t i", i=2, t=PACK)
+            src = values[:].rearrange("p t (c i) -> p c t i", i=2)
             if c < 2:
                 nc.scalar.activation(dst, src, COPY)
             else:
@@ -197,9 +209,8 @@ def tile_picked_yinvent_sub_po_kernel(tc, x_words, x_scales, w1, w2, e_words, e_
         q4 = quantize("q4", dealt[3][:], 512)
         count = len(CHUNKS)
         look_up(0)
+        look_up(1)
         for c in range(count + 2):
-            if c + 1 < count:
-                look_up(c + 1)
             if c < count:
                 times_supplier(c)
             if 1 <= c <= count:
@@ -212,6 +223,8 @@ def tile_picked_yinvent_sub_po_kernel(tc, x_words, x_scales, w1, w2, e_words, e_
                 times_substitute(c)
             if c >= 2:
                 planes(c - 2)
+            if 1 <= c < count - 1:
+                look_up(c + 1)
         for q in range(4):
             queue = nc.sync if q % 2 == 0 else nc.scalar
             queue.dma_start(out_2[0, 4 * q : 4 * q + 4, :].bitcast(I32), out_scales[32 * q : 32 * q + 4, :].bitcast(I32))

from contextlib import ExitStack

import concourse.mybir as mybir

F32 = mybir.dt.float32
BF16 = mybir.dt.bfloat16
I32 = mybir.dt.int32
U32 = mybir.dt.uint32
U16 = mybir.dt.uint16
U8 = mybir.dt.uint8
FP8X4 = mybir.dt.float8_e4m3fn_x4
MULT = mybir.AluOpType.mult
ADD = mybir.AluOpType.add
COPY = mybir.ActivationFunctionType.Copy

P = 128
PACK = 4
TABLE = 1024
PICKED = 512
ORDERS = 1024
CHUNKS = (256, 384, 256, 128)
SPARE = 0
RING = 3
FLOPS = 2 * 512 * 512 * (3 * PICKED + ORDERS)


def tile_picked_yinvent_sub_po_kernel(tc, x_words, x_scales, w1, w2, e_words, e_scales, w3, unit, w4, offs, sup, itm, sp, sb2, out_0, out_1, out_2):
    nc = tc.nc
    with ExitStack() as ctx:
        keep = ctx.enter_context(tc.tile_pool(name="keep", bufs=1))
        psum = ctx.enter_context(tc.psum_pool(name="psum", bufs=4))

        def load_list(name, src):
            t = keep.tile(list(src.shape), U16, name=name)
            nc.sync.dma_start(t[:], src)
            return t

        def load_words(name, src):
            t = keep.tile([P, TABLE], U32, name=name, align_bytes=64)
            nc.sync.dma_start(t[:].bitcast(I32), src[0].rearrange("p c r -> p (c r)").bitcast(I32))
            return t

        def load_scales(name, src, queue):
            t = keep.tile([P, TABLE], U8, name=name, align_bytes=64)
            nc.vector.memset(t[:].bitcast(I32), 0)
            for q in range(4):
                queue.dma_start(t[32 * q : 32 * q + 4, :].bitcast(I32), src[0, 4 * q : 4 * q + 4, :].bitcast(I32))
            return t

        def load_weight(name, src, c0, c1):
            t = keep.tile([P, PACK, c1 - c0], F32, name=name)
            nc.sync.dma_start(t[:], src.rearrange("(p j) c -> p j c", j=PACK)[:, :, c0:c1])
            return t

        def gather_codes(name, table, dtype, lst, tag=None):
            t = keep.tile([P, PICKED], dtype, name=name, tag=tag or name, align_bytes=64)
            nc.vector.tensor_copy(t[:], table[:].indirect(lst[:]))
            return t

        def deal(engine, dealt, raw, m0, m1):
            dst = dealt[:].rearrange("p (t m j) -> p m j t", t=PACK, j=PACK)[:, m0:m1, :, :]
            src = raw.rearrange("p j (m t) -> p m j t", t=PACK)
            if engine == "scalar":
                nc.scalar.activation(dst, src, COPY)
            else:
                nc.vector.tensor_copy(dst, src)

        def quantize(name, values, width, tags=None):
            tags = tags or (name + "_codes", name + "_scales")
            codes = keep.tile([P, width], U32, name=name + "_codes", tag=tags[0], align_bytes=64)
            scales = keep.tile([P, width], U8, name=name + "_scales", tag=tags[1], align_bytes=64)
            nc.vector.quantize_mx(out=codes[:].bitcast(FP8X4), scales=scales[:], in_=values)
            return codes, scales

        def product(dst, weight, t, codes, scales):
            cols = slice(P * t, P * (t + 1))
            nc.tensor.matmul_mx(out=dst, lhsT=weight[0][:, cols].bitcast(FP8X4), lhsT_scale=weight[1][:, cols],
                                rhs=codes.bitcast(FP8X4), rhs_scale=scales, start=True, stop=True)

        def first_layer(name, weight, codes, scales, factor):
            tiles = []
            for t in range(PACK):
                bank = psum.tile([P, PICKED], F32, name="first_bank")
                product(bank[:], weight, t, codes[:], scales[:])
                res = keep.tile([P, PICKED + SPARE], F32, name="%s%d" % (name, t))
                if factor is None:
                    nc.scalar.activation(res[:, :PICKED], bank[:], COPY)
                else:
                    nc.scalar.activation(res[:, :PICKED], bank[:], COPY, scale=factor[:, t : t + 1])
                tiles.append(res)
            return tiles

        offs_t = load_list("offs", offs)
        w1a = load_weight("w1a", w1, 0, 256)
        xs = load_scales("xs", x_scales, nc.sync)
        xw = load_words("xw", x_words)
        w1b = load_weight("w1b", w1, 256, 512)
        ew = load_words("ew", e_words)
        sup_t = load_list("sup", sup)
        es = load_scales("es", e_scales, nc.sync)
        w3r = load_weight("w3r", w3, 0, 512)
        w3a, w3b = w3r[:, :, 0:256], w3r[:, :, 256:512]
        itm_t = load_list("itm", itm)
        w2r = load_weight("w2r", w2, 0, 512)
        w2a, w2b = w2r[:, :, 0:256], w2r[:, :, 256:512]
        u = keep.tile([P, PACK], F32, name="u")
        nc.sync.dma_start(u[:], unit.rearrange("(p t) o -> p (t o)", t=PACK))
        sp_t = load_list("sp", sp)
        sb2_t = load_list("sb2", sb2)
        w4r = load_weight("w4r", w4, 0, 512)
        w4a, w4b = w4r[:, :, 0:256], w4r[:, :, 256:512]

        dealt = [keep.tile([P, 512 * PACK], BF16, name="dealt%d" % i, tag="dealt%d" % i, align_bytes=64) for i in range(4)]

        xs_p = gather_codes("xs_p", xs, U8, offs_t)
        xw_p = gather_codes("xw_p", xw, U32, offs_t)
        deal("scalar", dealt[0], w1a[:], 0, 64)
        deal("vector", dealt[0], w1b[:, :, 0:160], 64, 104)
        deal("scalar", dealt[0], w1b[:, :, 160:256], 104, 128)
        q1 = quantize("q1", dealt[0][:], 512)
        ew_p = gather_codes("ew_p", ew, U32, sup_t, "dealt0")
        es_p = gather_codes("es_p", es, U8, sup_t)
        neg_u = keep.tile([P, PACK], F32, name="neg_u")
        nc.vector.tensor_scalar(neg_u[:], u[:], -1.0, None, MULT)
        y = first_layer("y", q1, xw_p, xs_p, None)
        deal("vector", dealt[1], w3r[:], 0, 128)
        q3 = quantize("q3", dealt[1][:], 512)
        ye = first_layer("ye", q3, ew_p, es_p, u)
        deal("vector", dealt[2], w2r[:], 0, 128)
        q2 = quantize("q2", dealt[2][:], 512, ("ring2", "ring1"))
        z = first_layer("z", q2, xw_p, xs_p, neg_u)

        out_codes = keep.tile([P, ORDERS], U32, name="out_codes", align_bytes=64)
        out_scales = keep.tile([P, ORDERS], U8, name="out_scales", align_bytes=64)
        out_rows = out_0.rearrange("(p t) r -> p t r", t=PACK)
        out_words = out_1[0].rearrange("p c r -> p (c r)").bitcast(I32)

        starts = [sum(CHUNKS[:c]) for c in range(len(CHUNKS))]
        state = {}

        def list_cols(c):
            return slice(starts[c] // 16, (starts[c] + CHUNKS[c]) // 16)

        def look_up(c):
            for name, lst, slot in (("a", itm_t, 2 * c), ("g", sb2_t, 2 * c + 1)):
                picked = keep.tile([P, PACK, CHUNKS[c]], F32, name="%s%d" % (name, c), tag="ring%d" % (slot % RING), align_bytes=64)
                for t in range(PACK):
                    nc.scalar.activation(picked[:, t, :], y[t][:].indirect(lst[:, list_cols(c)]), COPY)
                state[name, c] = picked
            if c >= len(CHUNKS) - 0:
                second = keep.tile([P, PACK, CHUNKS[c]], F32, name="second%d" % c, tag="b%d" % (c - 2))
                for t in range(PACK):
                    nc.scalar.activation(second[:, t, :], z[t][:].indirect(itm_t[:, list_cols(c)]), COPY)
                state["second", c] = second

        def times_supplier(c):
            b = keep.tile([P, PACK, CHUNKS[c]], F32, name="b%d" % c, tag="b%d" % c)
            for t in range(PACK):
                nc.vector.tensor_tensor(b[:, t, :], ye[t][:].indirect(sp_t[:, list_cols(c)]), state["a", c][:, t, :], MULT)
            state["b", c] = b

        def less_second(c):
            gap = keep.tile([P, PACK, CHUNKS[c]], F32, name="gap%d" % c)
            if c >= len(CHUNKS) - 0:
                nc.vector.tensor_tensor(gap[:], state["second", c][:], state["b", c][:], ADD)
            else:
                for t in range(PACK):
                    nc.vector.tensor_tensor(gap[:, t, :], z[t][:].indirect(itm_t[:, list_cols(c)]), state["b", c][:, t, :], ADD)
            state["gap", c] = gap

        def times_substitute(c):
            hid = keep.tile([P, CHUNKS[c] * PACK], BF16, name="hid%d" % c, align_bytes=64)
            nc.vector.tensor_tensor(hid[:].rearrange("p (c i t) -> p c t i", i=2, t=PACK),
                                    state["gap", c][:].rearrange("p t (c i) -> p c t i", i=2),
                                    state["g", c][:].rearrange("p t (c i) -> p c t i", i=2), MULT)
            state["hid", c] = hid

        def last_product(c):
            n, r0 = CHUNKS[c], starts[c]
            codes, scales = quantize("hq%d" % c, state["hid", c][:], n)
            res = keep.tile([P, PACK, n], F32, name="res%d" % c)
            per_bank = 512 // n
            for t0 in range(0, PACK, per_bank):
                bank = psum.tile([P, per_bank, n], F32, name="last_bank")
                for t in range(per_bank):
                    for lo, hi in (((0, 256), (256, n)) if n == 384 else ((0, n),)):
                        if hi > lo:
                            product(bank[:, t, lo:hi], q4, t0 + t, codes[:, lo:hi], scales[:, lo:hi])
                nc.scalar.activation(res[:, t0 : t0 + per_bank, :], bank[:], COPY)
                nc.sync.dma_start(out_rows[:, t0 : t0 + per_bank, r0 : r0 + n], res[:, t0 : t0 + per_bank, :])
            state["res", c] = res

        def round_result(c, values):
            rounded = keep.tile([P, CHUNKS[c] * PACK], BF16, name="rounded%d" % c, align_bytes=64)
            dst = rounded[:].rearrange("p (c i t) -> p c t i", i=2, t=PACK)
            src = values[:].rearrange("p t (c i) -> p c t i", i=2)
            if c < 2:
                nc.scalar.activation(dst, src, COPY)
            else:
                nc.vector.tensor_copy(dst, src)
            state["rounded", c] = rounded

        def planes(c):
            n, r0 = CHUNKS[c], starts[c]
            nc.vector.quantize_mx(out=out_codes[:, r0 : r0 + n].bitcast(FP8X4), scales=out_scales[:, r0 : r0 + n], in_=state["rounded", c][:])
            nc.sync.dma_start(out_words[:, r0 : r0 + n], out_codes[:, r0 : r0 + n].bitcast(I32))

        deal("vector", dealt[3], w4r[:], 0, 128)
        q4 = quantize("q4", dealt[3][:], 512)
        count = len(CHUNKS)
        look_up(0)
        look_up(1)
        for c in range(count + 2):
            if c < count:
                times_supplier(c)
            if 1 <= c <= count:
                last_product(c - 1)
            if c < count:
                less_second(c)
            if c >= 2:
                round_result(c - 2, state["res", c - 2])
            if c < count:
                times_substitute(c)
            if c >= 2:
                planes(c - 2)
            if 1 <= c < count - 1:
                look_up(c + 1)
        for q in range(4):
            queue = nc.sync if q % 2 == 0 else nc.scalar
            queue.dma_start(out_2[0, 4 * q : 4 * q + 4, :].bitcast(I32), out_scales[32 * q : 32 * q + 4, :].bitcast(I32))
